import numpy as np
import ml_dtypes


def mxq(x, axis, fmt="e4m3"):
    dtype, down = {"e4m3": (ml_dtypes.float8_e4m3fn, 7), "e5m2": (ml_dtypes.float8_e5m2, 14)}[fmt]
    v = np.moveaxis(np.asarray(x, np.float32).astype(ml_dtypes.bfloat16).astype(np.float64), axis, -1)
    blocks = v.reshape(v.shape[:-1] + (-1, 32))
    amax = np.abs(blocks).max(-1, keepdims=True)
    byte = np.maximum(np.where(amax > 0, np.frexp(amax)[1] - 1 + 127, 0) - down, 1)
    scale = np.exp2(byte - 127.0)
    codes = (blocks / scale).astype(np.float32).astype(dtype).astype(np.float64)
    return np.moveaxis((codes * scale).reshape(v.shape), -1, axis)


WIDE = False


def mx_kscale(k):
    if not WIDE:
        return np.ones(k)
    levels = np.array([10, -10, 5, -5, 0])
    if k % 512:
        return np.exp2(np.random.permutation(np.resize(levels, k // 32))).repeat(32)
    a = np.empty((k // 512, 16))
    for p in range(k // 512):
        a[p, :8] = np.random.permutation(np.resize(levels, 8))
        for g in range(8):
            far = levels[np.abs(levels - a[p, g]) >= 10]
            a[p, g + 8] = far[np.random.randint(len(far))]
    return np.exp2(a.ravel()).repeat(32)


def f64(x):
    return np.asarray(x).astype(np.float64)


def striped(idx):
    return np.tile(idx.reshape(-1, 16).T, (8, 1)).astype(np.uint16)


def unstriped(offs):
    return offs[:16].T.reshape(-1).astype(np.int64)


E2M1 = np.array([0.0, 0.5, 1.0, 1.5, 2.0, 3.0, 4.0, 6.0, -0.0, -0.5, -1.0, -1.5, -2.0, -3.0, -4.0, -6.0])


def pack_weight(w, fmt):
    k, n = w.shape
    w = f64(np.asarray(w, np.float32).astype(ml_dtypes.bfloat16)).reshape(k // 32, 32, n)
    amax = np.abs(w).max(1)
    if fmt == "e4m3":
        byte = np.frexp(amax)[1] - 1 + 127 - 7
    else:
        mant, ex = np.frexp(amax / 6.0)
        byte = np.where(mant > 0.5, ex, ex - 1) + 127
    byte = np.clip(np.where(amax > 0, byte, 1), 1, 254)
    scaled = (w * np.exp2(127.0 - byte)[:, None, :]).reshape(k, n).astype(np.float32)
    by_word = np.ascontiguousarray(scaled.reshape(k // 512, 128, 4, n).transpose(0, 1, 3, 2))
    if fmt == "e4m3":
        words = by_word.astype(ml_dtypes.float8_e4m3fn).view(np.uint8)
    else:
        c = by_word.astype(ml_dtypes.float4_e2m1fn).view(np.uint8) & 0xF
        words = (c[..., 0::2] | (c[..., 1::2] << 4)).reshape(k // 512, 128, 2 * n)
    return np.ascontiguousarray(words), np.ascontiguousarray(byte.astype(np.uint8).reshape(k // 512, 16, n))


def unpack_weight(words, scales, fmt):
    g, _, n = scales.shape
    words = np.ascontiguousarray(words).reshape(g, 128, n, -1)
    if fmt == "e4m3":
        vals = words.view(ml_dtypes.float8_e4m3fn).astype(np.float64)
    else:
        nib = np.empty((g, 128, n, 4), np.uint8)
        nib[..., 0::2] = words & 0xF
        nib[..., 1::2] = words >> 4
        vals = E2M1[nib]
    vals = vals * np.repeat(np.exp2(scales.astype(np.float64) - 127.0), 8, axis=1)[..., None]
    return vals.transpose(0, 1, 3, 2).reshape(g * 512, n)


def planes(y):
    n, m = y.shape
    v = y.astype(np.float32).astype(ml_dtypes.bfloat16).astype(np.float64).reshape(n // 32, 32, m)
    top = np.abs(v).max(1)
    byte = np.clip(np.where(top > 0, np.frexp(top)[1] - 1 + 127 - 7, 1), 1, 254)
    codes = (v * np.exp2(127.0 - byte)[:, None, :]).reshape(n, m).astype(np.float32).astype(ml_dtypes.float8_e4m3fn).view(np.uint8)
    words = codes.reshape(n // 512, 128, 4, m).transpose(0, 1, 3, 2)
    return np.ascontiguousarray(words), np.ascontiguousarray(byte.astype(np.uint8).reshape(n // 512, 16, m))


K, T, E1, C1, E2, C2, H = 512, 768, 6, 128, 3, 256, 512
N = 512


def deal(E, C):
    slot_token = np.random.permutation(T)
    return slot_token, None, np.random.uniform(0.2, 1.0, T)


def by_expert(wq, xq, E, C):
    return np.concatenate([wq[e].T @ xq[:, e * C:(e + 1) * C] for e in range(E)], axis=1)


def setup_inputs():
    n = np.random.standard_normal
    s = mx_kscale(K)
    u = mx_kscale(H)
    slots1, pos1, g1 = deal(E1, C1)
    slots2, pos2, g2 = deal(E2, C2)
    x = pack_weight(n((K, T)) * s[:, None], "e4m3")
    w1 = [pack_weight(m, "e2m1") for m in n((E1, K, H)) / np.sqrt(K) / s[None, :, None] * u]
    w2 = [pack_weight(m, "e2m1") for m in n((E2, H, N)) / np.sqrt(H) / u[None, :, None]]
    return {
        "x_words": x[0],
        "x_scales": x[1],
        "w1_words": np.stack([m[0] for m in w1]),
        "w1_scales": np.stack([m[1] for m in w1]),
        "w2_words": np.stack([m[0] for m in w2]),
        "w2_scales": np.stack([m[1] for m in w2]),
        "gate1": (np.tile(g1, (128, 1))).astype(np.float32),
        "gate2": (np.tile(g2, (128, 1))).astype(np.float32),
        "offs": striped(slots1),
        "offs2": striped(slots2),
    }


def reference(x_words, x_scales, w1_words, w1_scales, w2_words, w2_scales, gate1, gate2, offs, offs2):
    w1 = np.stack([unpack_weight(w1_words[e], w1_scales[e], "e2m1") for e in range(E1)])
    w2 = np.stack([unpack_weight(w2_words[e], w2_scales[e], "e2m1") for e in range(E2)])
    idx, idx2 = unstriped(offs), unstriped(offs2)
    xq = unpack_weight(x_words, x_scales, "e4m3")[:, idx]
    h = by_expert(w1, xq, E1, C1)
    c = np.zeros((H, T))
    c[:, idx] = f64(gate1[:1]) * h
    y = by_expert(w2, mxq(c[:, idx2], 0, "e4m3"), E2, C2)
    out = np.zeros((N, T))
    out[:, idx2] = f64(gate2[:1]) * y
    out_0 = out
    return (out_0,) + planes(out_0)

@@ -1,0 +1,215 @@
+from contextlib import ExitStack
+
+import concourse.mybir as mybir
+from concourse.masks import make_identity
+
+F32 = mybir.dt.float32
+BF16 = mybir.dt.bfloat16
+I32 = mybir.dt.int32
+U32 = mybir.dt.uint32
+U16 = mybir.dt.uint16
+U8 = mybir.dt.uint8
+FP8X4 = mybir.dt.float8_e4m3fn_x4
+FP4X4 = mybir.dt.float4_e2m1fn_x4
+COPY = mybir.ActivationFunctionType.Copy
+
+P = 128
+T = 768
+D = 512
+E1, E2 = 6, 3
+BLOCKS = T // P
+PER_COL = 16
+
+FLOPS = 2 * 2 * D * D * T
+
+X_GATHERS = (1, 2, 3)
+W1_LOADS = (2, 4)
+C_SCATTERS = (1, 1, 2, 2)
+C_GATHERS = (1, 1, 2, 2)
+Y_SCATTERS = (1, 1, 4)
+OUT_COLS = 256
+
+
+def runs(sizes):
+    first = 0
+    out = []
+    for n in sizes:
+        out.append((first, n))
+        first = first + n
+    return out
+
+
+def find(groups, block):
+    for g, (first, n) in enumerate(groups):
+        if first <= block < first + n:
+            return g, block - first
+
+
+def entries(lst, first, n):
+    return lst[:, first * P // PER_COL : (first + n) * P // PER_COL]
+
+
+def tile_moe_ser_none_kernel(
+    tc, x_words, x_scales, w1_words, w1_scales, w2_words, w2_scales, gate1, gate2, offs, offs2, out_0, out_1, out_2
+):
+    nc = tc.nc
+    with ExitStack() as ctx:
+        keep = ctx.enter_context(tc.tile_pool(name="keep", bufs=1))
+        ring = ctx.enter_context(tc.tile_pool(name="ring", bufs=2))
+        psum = ctx.enter_context(tc.psum_pool(name="psum", bufs=2))
+
+        list1 = keep.tile([P, T // PER_COL], U16, name="list1")
+        list2 = keep.tile([P, T // PER_COL], U16, name="list2")
+        xw = keep.tile([P, T], U32, name="xw", align_bytes=64)
+        xs = keep.tile([P, T], U8, name="xs", align_bytes=64)
+        w1s = keep.tile([P, E1, D], U8, name="w1s", align_bytes=64)
+        w2s = keep.tile([P, E2, D], U8, name="w2s", align_bytes=64)
+        w1_groups = runs(W1_LOADS)
+        w1w = [keep.tile([P, w1_groups[0][1], 2 * D], U8, name="w1w0", align_bytes=64)]
+        ident = keep.tile([P, P], F32, name="ident")
+        gate_cols = [keep.tile([P, 8], F32, name=f"gate_cols{l}") for l in range(2)]
+
+        nc.vector.memset(w1s[:].bitcast(I32), 0)
+        nc.vector.memset(w2s[:].bitcast(I32), 0)
+        make_identity(nc, ident[:])
+
+        def load_weights(tile, words, first, n):
+            nc.sync.dma_start(tile[:].bitcast(I32), words[first : first + n, 0].rearrange("e p c -> p e c").bitcast(I32))
+
+        def load_weight_scales(tile, scales):
+            for q in range(4):
+                nc.sync.dma_start(
+                    tile[32 * q : 32 * q + 4].bitcast(I32),
+                    scales[:, 0, 4 * q : 4 * q + 4, :].rearrange("e r c -> r e c").bitcast(I32),
+                )
+
+        def load_gate(layer, gate):
+            rows = gate.rearrange("r (b u) -> (r b) u", u=P)
+            gate_rows = keep.tile([P, P], F32, name=f"gate_rows{layer}", align_bytes=64)
+            nc.sync.dma_start(gate_rows[:], rows[0:P, :])
+            turned = psum.tile([P, 4, P], F32, name="turned")
+            nc.tensor.transpose(turned[:, 0, :], gate_rows[:], ident[:])
+            nc.scalar.activation(gate_cols[layer][:], turned[:, 0, 0:8], COPY)
+
+        nc.sync.dma_start(list1[:], offs)
+        for q in range(4):
+            rows = x_scales[0, 4 * q : 4 * q + 4, :].bitcast(I32)
+            nc.sync.dma_start(xs[32 * q : 32 * q + 32, :].bitcast(I32), rows.unsqueeze(0).to_broadcast([8, 4, T // 4]))
+        nc.sync.dma_start(xw[:].bitcast(I32), x_words[0].rearrange("p t d -> p (t d)").bitcast(I32))
+        load_weights(w1w[0], w1_words, *w1_groups[0])
+        load_gate(0, gate1)
+        nc.sync.dma_start(list2[:], offs2)
+        load_weight_scales(w1s, w1_scales)
+        w1w.append(keep.tile([P, w1_groups[1][1], 2 * D], U8, name="w1w1", align_bytes=64))
+        load_weights(w1w[1], w1_words, *w1_groups[1])
+        load_weight_scales(w2s, w2_scales)
+
+        x_groups = runs(X_GATHERS)
+        xg = []
+        for g, (first, n) in enumerate(x_groups):
+            words = keep.tile([P, n * P], U32, name=f"xg_words{g}", align_bytes=64)
+            scales = keep.tile([P, n * P], U8, name=f"xg_scales{g}", align_bytes=64)
+            nc.vector.tensor_copy(words[:], xw[:].indirect(entries(list1, first, n)))
+            nc.vector.tensor_copy(scales[:], xs[:].indirect(entries(list1, first, n)))
+            xg.append((words, scales))
+
+        c_pairs = [keep.tile([P, T], F32, name=f"c_pairs{u}") for u in range(2)]
+        for g, (first, n) in enumerate(runs(C_SCATTERS)):
+            slot_pairs = keep.tile([P, 2, n * P], F32, name=f"slot_pairs{g}")
+            for j in range(n):
+                e = first + j
+                xi, xj = find(x_groups, e)
+                wi, wj = find(w1_groups, e)
+                cols = slice(xj * P, (xj + 1) * P)
+                acc = psum.tile([P, D], F32, name="acc")
+                nc.tensor.matmul_mx(
+                    out=acc[:],
+                    lhsT=xg[xi][0][:, cols].bitcast(FP8X4),
+                    lhsT_scale=xg[xi][1][:, cols],
+                    rhs=w1w[wi][:, wj, :].bitcast(FP4X4),
+                    rhs_scale=w1s[:, e, :],
+                    start=True,
+                    stop=True,
+                )
+                c_rows = ring.tile([P, 2, P, 2], BF16, name="c_rows")
+                nc.scalar.activation(
+                    c_rows[:], acc[:].rearrange("s (p u h) -> s u p h", u=2, h=2), COPY, scale=gate_cols[0][:, e : e + 1]
+                )
+                c_row_words = c_rows[:].rearrange("s u p h -> s (u p h)").bitcast(F32)
+                turned = psum.tile([P, 4, P], F32, name="turned")
+                for u in range(2):
+                    nc.tensor.transpose(turned[:, u, :], c_row_words[:, u * P : (u + 1) * P], ident[:])
+                nc.scalar.copy(slot_pairs[:, :, j * P : (j + 1) * P], turned[:, 0:2, :])
+            for u in range(2):
+                nc.vector.tensor_copy(c_pairs[u][:].indirect(entries(list1, first, n)), slot_pairs[:, u, :])
+
+        load_gate(1, gate2)
+        w2w = keep.tile([P, E2, 2 * D], U8, name="w2w", align_bytes=64)
+        load_weights(w2w, w2_words, 0, E2)
+
+        c_groups = runs(C_GATHERS)
+        cq = []
+        for g, (first, n) in enumerate(c_groups):
+            grouped = keep.tile([P, n * P * 4], BF16, name=f"c_grouped{g}", align_bytes=64)
+            codes = keep.tile([P, n * P], U32, name=f"c_codes{g}", align_bytes=64)
+            scales = keep.tile([P, n * P], U8, name=f"c_scales{g}", align_bytes=64)
+            grouped_words = grouped[:].bitcast(U32).rearrange("p (m u) -> p m u", u=2)
+            for u in range(2):
+                nc.vector.tensor_copy(grouped_words[:, :, u], c_pairs[u][:].bitcast(U32).indirect(entries(list2, first, n)))
+            nc.vector.quantize_mx(out=codes[:].bitcast(FP8X4), scales=scales[:], in_=grouped[:])
+            cq.append((codes, scales))
+
+        y_tokens = [keep.tile([P, T], F32, name=f"y_tokens{t}") for t in range(4)]
+        for g, (first, n) in enumerate(runs(Y_SCATTERS)):
+            y_slots = keep.tile([P, 4, n * P], F32, name=f"y_slots{g}")
+            for j in range(n):
+                b = first + j
+                f = b * E2 // BLOCKS
+                ci, cj = find(c_groups, b)
+                cols = slice(cj * P, (cj + 1) * P)
+                acc = psum.tile([P, D], F32, name="acc")
+                nc.tensor.matmul_mx(
+                    out=acc[:],
+                    lhsT=cq[ci][0][:, cols].bitcast(FP8X4),
+                    lhsT_scale=cq[ci][1][:, cols],
+                    rhs=w2w[:, f, :].bitcast(FP4X4),
+                    rhs_scale=w2s[:, f, :],
+                    start=True,
+                    stop=True,
+                )
+                y_rows = ring.tile([P, 4, P], F32, name="y_rows")
+                nc.scalar.activation(
+                    y_rows[:], acc[:].rearrange("s (p t) -> s t p", t=4), COPY, scale=gate_cols[1][:, b : b + 1]
+                )
+                turned = psum.tile([P, 4, P], F32, name="turned")
+                for t in range(4):
+                    nc.tensor.transpose(turned[:, t, :], y_rows[:, t, :], ident[:])
+                nc.scalar.copy(y_slots[:, :, j * P : (j + 1) * P], turned[:])
+            for t in range(4):
+                nc.vector.tensor_copy(y_tokens[t][:].indirect(entries(list2, first, n)), y_slots[:, t, :])
+
+        pieces = T // OUT_COLS
+        out_rows = out_0.rearrange("(p t) c -> p t c", t=4)
+        out_grouped = [keep.tile([P, OUT_COLS, 4], BF16, name=f"out_grouped{k}", align_bytes=64) for k in range(pieces)]
+        out_scales = keep.tile([P, T], U8, name="out_scales", align_bytes=64)
+        for t in range(4):
+            nc.sync.dma_start(out_rows[:, t, :], y_tokens[t][:])
+            for k in range(pieces):
+                src = y_tokens[t][:, k * OUT_COLS : (k + 1) * OUT_COLS]
+                if t == 3 and k < pieces - 1:
+                    nc.vector.tensor_copy(out_grouped[k][:, :, t], src)
+                elif t == 2 and k < pieces - 1:
+                    nc.scalar.copy(out_grouped[k][:, :, 2:4], src.unsqueeze(2).to_broadcast([P, OUT_COLS, 2]))
+                else:
+                    nc.scalar.copy(out_grouped[k][:, :, t], src)
+        out_words = out_1[0].rearrange("p c d -> p (c d)").bitcast(I32)
+        for k in range(pieces):
+            cols = slice(k * OUT_COLS, (k + 1) * OUT_COLS)
+            codes = keep.tile([P, OUT_COLS], U32, name=f"out_codes{k}", align_bytes=64)
+            nc.vector.quantize_mx(
+                out=codes[:].bitcast(FP8X4), scales=out_scales[:, cols], in_=out_grouped[k][:].rearrange("p c t -> p (c t)")
+            )
+            nc.sync.dma_start(out_words[:, cols], codes[:].bitcast(I32))
+        for q in range(4):
+            queue = nc.scalar if q % 2 else nc.sync
+            queue.dma_start(out_2[0, 4 * q : 4 * q + 4, :].bitcast(I32), out_scales[32 * q : 32 * q + 4, :].bitcast(I32))

@@ -23,7 +23,7 @@ PER_COL = 16
 FLOPS = 2 * 2 * D * D * T
 
 X_GATHERS = (1, 2, 3)
-W1_LOADS = (2, 4)
+W1_LOADS = (1, 2, 3)
 C_SCATTERS = (1, 1, 2, 2)
 C_GATHERS = (1, 1, 2, 2)
 Y_SCATTERS = (1, 1, 4)
@@ -56,7 +56,7 @@ def tile_moe_ser_none_kernel(
     with ExitStack() as ctx:
         keep = ctx.enter_context(tc.tile_pool(name="keep", bufs=1))
         ring = ctx.enter_context(tc.tile_pool(name="ring", bufs=2))
-        psum = ctx.enter_context(tc.psum_pool(name="psum", bufs=2))
+        psum = ctx.enter_context(tc.psum_pool(name="psum", bufs=4))
 
         list1 = keep.tile([P, T // PER_COL], U16, name="list1")
         list2 = keep.tile([P, T // PER_COL], U16, name="list2")
@@ -100,8 +100,9 @@ def tile_moe_ser_none_kernel(
         load_gate(0, gate1)
         nc.sync.dma_start(list2[:], offs2)
         load_weight_scales(w1s, w1_scales)
-        w1w.append(keep.tile([P, w1_groups[1][1], 2 * D], U8, name="w1w1", align_bytes=64))
-        load_weights(w1w[1], w1_words, *w1_groups[1])
+        for g in range(1, len(w1_groups)):
+            w1w.append(keep.tile([P, w1_groups[g][1], 2 * D], U8, name=f"w1w{g}", align_bytes=64))
+            load_weights(w1w[g], w1_words, *w1_groups[g])
         load_weight_scales(w2s, w2_scales)
 
         x_groups = runs(X_GATHERS)
@@ -121,7 +122,7 @@ def tile_moe_ser_none_kernel(
                 xi, xj = find(x_groups, e)
                 wi, wj = find(w1_groups, e)
                 cols = slice(xj * P, (xj + 1) * P)
-                acc = psum.tile([P, D], F32, name="acc")
+                acc = psum.tile([P, D], F32, name="acc", bufs=2)
                 nc.tensor.matmul_mx(
                     out=acc[:],
                     lhsT=xg[xi][0][:, cols].bitcast(FP8X4),
@@ -132,14 +133,16 @@ def tile_moe_ser_none_kernel(
                     stop=True,
                 )
                 c_rows = ring.tile([P, 2, P, 2], BF16, name="c_rows")
-                nc.scalar.activation(
-                    c_rows[:], acc[:].rearrange("s (p u h) -> s u p h", u=2, h=2), COPY, scale=gate_cols[0][:, e : e + 1]
-                )
                 c_row_words = c_rows[:].rearrange("s u p h -> s (u p h)").bitcast(F32)
-                turned = psum.tile([P, 4, P], F32, name="turned")
-                for u in range(2):
-                    nc.tensor.transpose(turned[:, u, :], c_row_words[:, u * P : (u + 1) * P], ident[:])
-                nc.scalar.copy(slot_pairs[:, :, j * P : (j + 1) * P], turned[:, 0:2, :])
+                sums = acc[:].rearrange("s (p u h) -> s u p h", u=2, h=2)
+                step = 1 if e == 0 else 2
+                for u0 in range(0, 2, step):
+                    part = slice(u0, u0 + step)
+                    nc.scalar.activation(c_rows[:, part], sums[:, part], COPY, scale=gate_cols[0][:, e : e + 1])
+                    turned = psum.tile([P, 4, P], F32, name="turned")
+                    for u in range(u0, u0 + step):
+                        nc.tensor.transpose(turned[:, u, :], c_row_words[:, u * P : (u + 1) * P], ident[:])
+                    nc.scalar.copy(slot_pairs[:, part, j * P : (j + 1) * P], turned[:, part, :])
             for u in range(2):
                 nc.vector.tensor_copy(c_pairs[u][:].indirect(entries(list1, first, n)), slot_pairs[:, u, :])
 
@@ -150,7 +153,7 @@ def tile_moe_ser_none_kernel(
         c_groups = runs(C_GATHERS)
         cq = []
         for g, (first, n) in enumerate(c_groups):
-            grouped = keep.tile([P, n * P * 4], BF16, name=f"c_grouped{g}", align_bytes=64)
+            grouped = ring.tile([P, n * P * 4], BF16, name="c_grouped", align_bytes=64)
             codes = keep.tile([P, n * P], U32, name=f"c_codes{g}", align_bytes=64)
             scales = keep.tile([P, n * P], U8, name=f"c_scales{g}", align_bytes=64)
             grouped_words = grouped[:].bitcast(U32).rearrange("p (m u) -> p m u", u=2)
@@ -167,7 +170,7 @@ def tile_moe_ser_none_kernel(
                 f = b * E2 // BLOCKS
                 ci, cj = find(c_groups, b)
                 cols = slice(cj * P, (cj + 1) * P)
-                acc = psum.tile([P, D], F32, name="acc")
+                acc = psum.tile([P, D], F32, name="acc", bufs=2)
                 nc.tensor.matmul_mx(
                     out=acc[:],
                     lhsT=cq[ci][0][:, cols].bitcast(FP8X4),
@@ -178,13 +181,15 @@ def tile_moe_ser_none_kernel(
                     stop=True,
                 )
                 y_rows = ring.tile([P, 4, P], F32, name="y_rows")
-                nc.scalar.activation(
-                    y_rows[:], acc[:].rearrange("s (p t) -> s t p", t=4), COPY, scale=gate_cols[1][:, b : b + 1]
-                )
-                turned = psum.tile([P, 4, P], F32, name="turned")
-                for t in range(4):
-                    nc.tensor.transpose(turned[:, t, :], y_rows[:, t, :], ident[:])
-                nc.scalar.copy(y_slots[:, :, j * P : (j + 1) * P], turned[:])
+                sums = acc[:].rearrange("s (p t) -> s t p", t=4)
+                step = 1 if b == 0 else 4
+                for t0 in range(0, 4, step):
+                    part = slice(t0, t0 + step)
+                    nc.scalar.activation(y_rows[:, part], sums[:, part], COPY, scale=gate_cols[1][:, b : b + 1])
+                    turned = psum.tile([P, 4, P], F32, name="turned")
+                    for t in range(t0, t0 + step):
+                        nc.tensor.transpose(turned[:, t, :], y_rows[:, t, :], ident[:])
+                    nc.scalar.copy(y_slots[:, part, j * P : (j + 1) * P], turned[:, part, :])
             for t in range(4):
                 nc.vector.tensor_copy(y_tokens[t][:].indirect(entries(list2, first, n)), y_slots[:, t, :])
 

@@ -23,10 +23,10 @@ PER_COL = 16
 FLOPS = 2 * 2 * D * D * T
 
 X_GATHERS = (1, 2, 3)
-W1_LOADS = (1, 2, 3)
-C_SCATTERS = (1, 1, 2, 2)
+W1_LOADS = (2, 4)
+C_SCATTERS = (1, 1, 1, 1, 2)
 C_GATHERS = (1, 1, 2, 2)
-Y_SCATTERS = (1, 1, 4)
+Y_SCATTERS = (1, 1, 1, 3)
 OUT_COLS = 256
 
 
@@ -62,25 +62,26 @@ def tile_moe_ser_none_kernel(
         list2 = keep.tile([P, T // PER_COL], U16, name="list2")
         xw = keep.tile([P, T], U32, name="xw", align_bytes=64)
         xs = keep.tile([P, T], U8, name="xs", align_bytes=64)
-        w1s = keep.tile([P, E1, D], U8, name="w1s", align_bytes=64)
         w2s = keep.tile([P, E2, D], U8, name="w2s", align_bytes=64)
         w1_groups = runs(W1_LOADS)
         w1w = [keep.tile([P, w1_groups[0][1], 2 * D], U8, name="w1w0", align_bytes=64)]
+        w1s = [keep.tile([P, n, D], U8, name=f"w1s{g}", align_bytes=64) for g, (first, n) in enumerate(w1_groups)]
         ident = keep.tile([P, P], F32, name="ident")
         gate_cols = [keep.tile([P, 8], F32, name=f"gate_cols{l}") for l in range(2)]
 
-        nc.vector.memset(w1s[:].bitcast(I32), 0)
+        for tile in w1s:
+            nc.vector.memset(tile[:].bitcast(I32), 0)
         nc.vector.memset(w2s[:].bitcast(I32), 0)
         make_identity(nc, ident[:])
 
         def load_weights(tile, words, first, n):
             nc.sync.dma_start(tile[:].bitcast(I32), words[first : first + n, 0].rearrange("e p c -> p e c").bitcast(I32))
 
-        def load_weight_scales(tile, scales):
+        def load_weight_scales(tile, scales, first, n):
             for q in range(4):
                 nc.sync.dma_start(
                     tile[32 * q : 32 * q + 4].bitcast(I32),
-                    scales[:, 0, 4 * q : 4 * q + 4, :].rearrange("e r c -> r e c").bitcast(I32),
+                    scales[first : first + n, 0, 4 * q : 4 * q + 4, :].rearrange("e r c -> r e c").bitcast(I32),
                 )
 
         def load_gate(layer, gate):
@@ -99,11 +100,12 @@ def tile_moe_ser_none_kernel(
         load_weights(w1w[0], w1_words, *w1_groups[0])
         load_gate(0, gate1)
         nc.sync.dma_start(list2[:], offs2)
-        load_weight_scales(w1s, w1_scales)
+        for g, (first, n) in enumerate(w1_groups):
+            load_weight_scales(w1s[g], w1_scales, first, n)
         for g in range(1, len(w1_groups)):
             w1w.append(keep.tile([P, w1_groups[g][1], 2 * D], U8, name=f"w1w{g}", align_bytes=64))
             load_weights(w1w[g], w1_words, *w1_groups[g])
-        load_weight_scales(w2s, w2_scales)
+        load_weight_scales(w2s, w2_scales, 0, E2)
 
         x_groups = runs(X_GATHERS)
         xg = []
@@ -128,7 +130,7 @@ def tile_moe_ser_none_kernel(
                     lhsT=xg[xi][0][:, cols].bitcast(FP8X4),
                     lhsT_scale=xg[xi][1][:, cols],
                     rhs=w1w[wi][:, wj, :].bitcast(FP4X4),
-                    rhs_scale=w1s[:, e, :],
+                    rhs_scale=w1s[wi][:, wj, :],
                     start=True,
                     stop=True,
                 )
@@ -163,8 +165,12 @@ def tile_moe_ser_none_kernel(
             cq.append((codes, scales))
 
         y_tokens = [keep.tile([P, T], F32, name=f"y_tokens{t}") for t in range(4)]
+        y_slots = keep.tile([P, 4, T], F32, name="y_slots")
+
+        def scatter_y(t, first, n):
+            nc.vector.tensor_copy(y_tokens[t][:].indirect(entries(list2, first, n)), y_slots[:, t, first * P : (first + n) * P])
+
         for g, (first, n) in enumerate(runs(Y_SCATTERS)):
-            y_slots = keep.tile([P, 4, n * P], F32, name=f"y_slots{g}")
             for j in range(n):
                 b = first + j
                 f = b * E2 // BLOCKS
@@ -189,9 +195,10 @@ def tile_moe_ser_none_kernel(
                     turned = psum.tile([P, 4, P], F32, name="turned")
                     for t in range(t0, t0 + step):
                         nc.tensor.transpose(turned[:, t, :], y_rows[:, t, :], ident[:])
-                    nc.scalar.copy(y_slots[:, part, j * P : (j + 1) * P], turned[:, part, :])
-            for t in range(4):
-                nc.vector.tensor_copy(y_tokens[t][:].indirect(entries(list2, first, n)), y_slots[:, t, :])
+                    nc.scalar.copy(y_slots[:, part, b * P : (b + 1) * P], turned[:, part, :])
+            for t in range(4 if first < 2 else 3):
+                scatter_y(t, first, n)
+        scatter_y(3, 2, BLOCKS - 2)
 
         pieces = T // OUT_COLS
         out_rows = out_0.rearrange("(p t) c -> p t c", t=4)
@@ -216,5 +223,4 @@ def tile_moe_ser_none_kernel(
             )
             nc.sync.dma_start(out_words[:, cols], codes[:].bitcast(I32))
         for q in range(4):
-            queue = nc.scalar if q % 2 else nc.sync
-            queue.dma_start(out_2[0, 4 * q : 4 * q + 4, :].bitcast(I32), out_scales[32 * q : 32 * q + 4, :].bitcast(I32))
+            nc.scalar.dma_start(out_2[0, 4 * q : 4 * q + 4, :].bitcast(I32), out_scales[32 * q : 32 * q + 4, :].bitcast(I32))

@@ -25,8 +25,9 @@ FLOPS = 2 * 2 * D * D * T
 X_GATHERS = (1, 2, 3)
 W1_LOADS = (2, 4)
 C_SCATTERS = (1, 1, 1, 1, 2)
-C_GATHERS = (1, 1, 2, 2)
-Y_SCATTERS = (1, 1, 1, 3)
+C_GATHERS = (1, 1, 4)
+EARLY = 2
+SINGLY = (6, 3, 3, 2)
 OUT_COLS = 256
 
 
@@ -99,9 +100,9 @@ def tile_moe_ser_none_kernel(
         nc.sync.dma_start(xw[:].bitcast(I32), x_words[0].rearrange("p t d -> p (t d)").bitcast(I32))
         load_weights(w1w[0], w1_words, *w1_groups[0])
         load_gate(0, gate1)
+        load_weight_scales(w1s[0], w1_scales, *w1_groups[0])
         nc.sync.dma_start(list2[:], offs2)
-        for g, (first, n) in enumerate(w1_groups):
-            load_weight_scales(w1s[g], w1_scales, first, n)
+        load_weight_scales(w1s[1], w1_scales, *w1_groups[1])
         for g in range(1, len(w1_groups)):
             w1w.append(keep.tile([P, w1_groups[g][1], 2 * D], U8, name=f"w1w{g}", align_bytes=64))
             load_weights(w1w[g], w1_words, *w1_groups[g])
@@ -154,15 +155,27 @@ def tile_moe_ser_none_kernel(
 
         c_groups = runs(C_GATHERS)
         cq = []
-        for g, (first, n) in enumerate(c_groups):
-            grouped = ring.tile([P, n * P * 4], BF16, name="c_grouped", align_bytes=64)
+        staged = {}
+
+        def quantize_c(g, grouped):
+            n = c_groups[g][1]
             codes = keep.tile([P, n * P], U32, name=f"c_codes{g}", align_bytes=64)
             scales = keep.tile([P, n * P], U8, name=f"c_scales{g}", align_bytes=64)
-            grouped_words = grouped[:].bitcast(U32).rearrange("p (m u) -> p m u", u=2)
-            for u in range(2):
-                nc.vector.tensor_copy(grouped_words[:, :, u], c_pairs[u][:].bitcast(U32).indirect(entries(list2, first, n)))
             nc.vector.quantize_mx(out=codes[:].bitcast(FP8X4), scales=scales[:], in_=grouped[:])
             cq.append((codes, scales))
+
+        for g, (first, n) in enumerate(c_groups):
+            windows = [c_pairs[u][:].bitcast(U32).indirect(entries(list2, first, n)) for u in range(2)]
+            if g < EARLY:
+                grouped = ring.tile([P, n * P * 4], BF16, name="c_grouped", tag="c_gathered", align_bytes=64)
+                grouped_words = grouped[:].bitcast(U32).rearrange("p (m u) -> p m u", u=2)
+                for u in range(2):
+                    nc.vector.tensor_copy(grouped_words[:, :, u], windows[u])
+                quantize_c(g, grouped)
+            else:
+                staged[g] = ring.tile([P, 2, n * P], U32, name="c_staged", tag="c_gathered", align_bytes=64)
+                for u in range(2):
+                    nc.vector.tensor_copy(staged[g][:, u, :], windows[u])
 
         y_tokens = [keep.tile([P, T], F32, name=f"y_tokens{t}") for t in range(4)]
         y_slots = keep.tile([P, 4, T], F32, name="y_slots")
@@ -170,35 +183,44 @@ def tile_moe_ser_none_kernel(
         def scatter_y(t, first, n):
             nc.vector.tensor_copy(y_tokens[t][:].indirect(entries(list2, first, n)), y_slots[:, t, first * P : (first + n) * P])
 
-        for g, (first, n) in enumerate(runs(Y_SCATTERS)):
-            for j in range(n):
-                b = first + j
-                f = b * E2 // BLOCKS
-                ci, cj = find(c_groups, b)
-                cols = slice(cj * P, (cj + 1) * P)
-                acc = psum.tile([P, D], F32, name="acc", bufs=2)
-                nc.tensor.matmul_mx(
-                    out=acc[:],
-                    lhsT=cq[ci][0][:, cols].bitcast(FP8X4),
-                    lhsT_scale=cq[ci][1][:, cols],
-                    rhs=w2w[:, f, :].bitcast(FP4X4),
-                    rhs_scale=w2s[:, f, :],
-                    start=True,
-                    stop=True,
-                )
-                y_rows = ring.tile([P, 4, P], F32, name="y_rows")
-                sums = acc[:].rearrange("s (p t) -> s t p", t=4)
-                step = 1 if b == 0 else 4
-                for t0 in range(0, 4, step):
-                    part = slice(t0, t0 + step)
-                    nc.scalar.activation(y_rows[:, part], sums[:, part], COPY, scale=gate_cols[1][:, b : b + 1])
-                    turned = psum.tile([P, 4, P], F32, name="turned")
-                    for t in range(t0, t0 + step):
-                        nc.tensor.transpose(turned[:, t, :], y_rows[:, t, :], ident[:])
-                    nc.scalar.copy(y_slots[:, part, b * P : (b + 1) * P], turned[:, part, :])
-            for t in range(4 if first < 2 else 3):
-                scatter_y(t, first, n)
-        scatter_y(3, 2, BLOCKS - 2)
+        for b in range(BLOCKS):
+            f = b * E2 // BLOCKS
+            ci, cj = find(c_groups, b)
+            cols = slice(cj * P, (cj + 1) * P)
+            acc = psum.tile([P, D], F32, name="acc", bufs=2)
+            nc.tensor.matmul_mx(
+                out=acc[:],
+                lhsT=cq[ci][0][:, cols].bitcast(FP8X4),
+                lhsT_scale=cq[ci][1][:, cols],
+                rhs=w2w[:, f, :].bitcast(FP4X4),
+                rhs_scale=w2s[:, f, :],
+                start=True,
+                stop=True,
+            )
+            sums = acc[:].rearrange("s (p t) -> s t p", t=4)
+            step = 1 if b == 0 else 4
+            for t0 in range(0, 4, step):
+                part = slice(t0, t0 + step)
+                if b == 0:
+                    y_rows = keep.tile([P, step, P], F32, name="y_row", tag=f"y_row{t0}", align_bytes=64)
+                else:
+                    y_rows = ring.tile([P, step, P], F32, name="y_rows")
+                nc.scalar.activation(y_rows[:], sums[:, part], COPY, scale=gate_cols[1][:, b : b + 1])
+                turned = psum.tile([P, 4, P], F32, name="turned")
+                for t in range(step):
+                    nc.tensor.transpose(turned[:, t, :], y_rows[:, t, :], ident[:])
+                nc.scalar.copy(y_slots[:, part, b * P : (b + 1) * P], turned[:, 0:step, :])
+                if b == 0 and t0 == 1:
+                    woven = keep.tile([P, c_groups[EARLY][1] * P * 4], BF16, name="c_woven", tag="y_row1", align_bytes=64)
+                    nc.scalar.copy(
+                        woven[:].bitcast(U32).rearrange("p (m u) -> p m u", u=2), staged[EARLY][:].rearrange("p u m -> p m u")
+                    )
+                    quantize_c(EARLY, woven)
+            for t in range(4):
+                if b < SINGLY[t]:
+                    scatter_y(t, b, 1)
+        for t in range(1, 4):
+            scatter_y(t, SINGLY[t], BLOCKS - SINGLY[t])
 
         pieces = T // OUT_COLS
         out_rows = out_0.rearrange("(p t) c -> p t c", t=4)
@@ -223,4 +245,5 @@ def tile_moe_ser_none_kernel(
             )
             nc.sync.dma_start(out_words[:, cols], codes[:].bitcast(I32))
         for q in range(4):
-            nc.scalar.dma_start(out_2[0, 4 * q : 4 * q + 4, :].bitcast(I32), out_scales[32 * q : 32 * q + 4, :].bitcast(I32))
+            queue = nc.sync if q == 3 else nc.scalar
+            queue.dma_start(out_2[0, 4 * q : 4 * q + 4, :].bitcast(I32), out_scales[32 * q : 32 * q + 4, :].bitcast(I32))

@@ -27,7 +27,7 @@ W1_LOADS = (2, 4)
 C_SCATTERS = (1, 1, 1, 1, 2)
 C_GATHERS = (1, 1, 4)
 EARLY = 2
-SINGLY = (6, 3, 3, 2)
+SINGLY = (3, 3, 3, 2)
 OUT_COLS = 256
 
 
@@ -219,7 +219,7 @@ def tile_moe_ser_none_kernel(
             for t in range(4):
                 if b < SINGLY[t]:
                     scatter_y(t, b, 1)
-        for t in range(1, 4):
+        for t in range(4):
             scatter_y(t, SINGLY[t], BLOCKS - SINGLY[t])
 
         pieces = T // OUT_COLS

from contextlib import ExitStack

import concourse.mybir as mybir
from concourse.masks import make_identity

F32 = mybir.dt.float32
BF16 = mybir.dt.bfloat16
I32 = mybir.dt.int32
U32 = mybir.dt.uint32
U16 = mybir.dt.uint16
U8 = mybir.dt.uint8
FP8X4 = mybir.dt.float8_e4m3fn_x4
FP4X4 = mybir.dt.float4_e2m1fn_x4
COPY = mybir.ActivationFunctionType.Copy

P = 128
T = 768
D = 512
E1, E2 = 6, 3
BLOCKS = T // P
PER_COL = 16

FLOPS = 2 * 2 * D * D * T

X_GATHERS = (1, 2, 3)
W1_LOADS = (2, 4)
C_SCATTERS = (1, 1, 1, 1, 2)
C_GATHERS = (1, 1, 4)
EARLY = 2
SINGLY = (3, 3, 3, 2)
OUT_COLS = 256


def runs(sizes):
    first = 0
    out = []
    for n in sizes:
        out.append((first, n))
        first = first + n
    return out


def find(groups, block):
    for g, (first, n) in enumerate(groups):
        if first <= block < first + n:
            return g, block - first


def entries(lst, first, n):
    return lst[:, first * P // PER_COL : (first + n) * P // PER_COL]


def tile_moe_ser_none_kernel(
    tc, x_words, x_scales, w1_words, w1_scales, w2_words, w2_scales, gate1, gate2, offs, offs2, out_0, out_1, out_2
):
    nc = tc.nc
    with ExitStack() as ctx:
        keep = ctx.enter_context(tc.tile_pool(name="keep", bufs=1))
        ring = ctx.enter_context(tc.tile_pool(name="ring", bufs=2))
        psum = ctx.enter_context(tc.psum_pool(name="psum", bufs=4))

        list1 = keep.tile([P, T // PER_COL], U16, name="list1")
        list2 = keep.tile([P, T // PER_COL], U16, name="list2")
        xw = keep.tile([P, T], U32, name="xw", align_bytes=64)
        xs = keep.tile([P, T], U8, name="xs", align_bytes=64)
        w2s = keep.tile([P, E2, D], U8, name="w2s", align_bytes=64)
        w1_groups = runs(W1_LOADS)
        w1w = [keep.tile([P, w1_groups[0][1], 2 * D], U8, name="w1w0", align_bytes=64)]
        w1s = [keep.tile([P, n, D], U8, name=f"w1s{g}", align_bytes=64) for g, (first, n) in enumerate(w1_groups)]
        ident = keep.tile([P, P], F32, name="ident")
        gate_cols = [keep.tile([P, 8], F32, name=f"gate_cols{l}") for l in range(2)]

        for tile in w1s:
            nc.vector.memset(tile[:].bitcast(I32), 0)
        nc.vector.memset(w2s[:].bitcast(I32), 0)
        make_identity(nc, ident[:])

        def load_weights(tile, words, first, n):
            nc.sync.dma_start(tile[:].bitcast(I32), words[first : first + n, 0].rearrange("e p c -> p e c").bitcast(I32))

        def load_weight_scales(tile, scales, first, n):
            for q in range(4):
                nc.sync.dma_start(
                    tile[32 * q : 32 * q + 4].bitcast(I32),
                    scales[first : first + n, 0, 4 * q : 4 * q + 4, :].rearrange("e r c -> r e c").bitcast(I32),
                )

        def load_gate(layer, gate):
            rows = gate.rearrange("r (b u) -> (r b) u", u=P)
            gate_rows = keep.tile([P, P], F32, name=f"gate_rows{layer}", align_bytes=64)
            nc.sync.dma_start(gate_rows[:], rows[0:P, :])
            turned = psum.tile([P, 4, P], F32, name="turned")
            nc.tensor.transpose(turned[:, 0, :], gate_rows[:], ident[:])
            nc.scalar.activation(gate_cols[layer][:], turned[:, 0, 0:8], COPY)

        nc.sync.dma_start(list1[:], offs)
        for q in range(4):
            rows = x_scales[0, 4 * q : 4 * q + 4, :].bitcast(I32)
            nc.sync.dma_start(xs[32 * q : 32 * q + 32, :].bitcast(I32), rows.unsqueeze(0).to_broadcast([8, 4, T // 4]))
        nc.sync.dma_start(xw[:].bitcast(I32), x_words[0].rearrange("p t d -> p (t d)").bitcast(I32))
        load_weights(w1w[0], w1_words, *w1_groups[0])
        load_gate(0, gate1)
        load_weight_scales(w1s[0], w1_scales, *w1_groups[0])
        nc.sync.dma_start(list2[:], offs2)
        load_weight_scales(w1s[1], w1_scales, *w1_groups[1])
        for g in range(1, len(w1_groups)):
            w1w.append(keep.tile([P, w1_groups[g][1], 2 * D], U8, name=f"w1w{g}", align_bytes=64))
            load_weights(w1w[g], w1_words, *w1_groups[g])
        load_weight_scales(w2s, w2_scales, 0, E2)

        x_groups = runs(X_GATHERS)
        xg = []
        for g, (first, n) in enumerate(x_groups):
            words = keep.tile([P, n * P], U32, name=f"xg_words{g}", align_bytes=64)
            scales = keep.tile([P, n * P], U8, name=f"xg_scales{g}", align_bytes=64)
            nc.vector.tensor_copy(words[:], xw[:].indirect(entries(list1, first, n)))
            nc.vector.tensor_copy(scales[:], xs[:].indirect(entries(list1, first, n)))
            xg.append((words, scales))

        c_pairs = [keep.tile([P, T], F32, name=f"c_pairs{u}") for u in range(2)]
        for g, (first, n) in enumerate(runs(C_SCATTERS)):
            slot_pairs = keep.tile([P, 2, n * P], F32, name=f"slot_pairs{g}")
            for j in range(n):
                e = first + j
                xi, xj = find(x_groups, e)
                wi, wj = find(w1_groups, e)
                cols = slice(xj * P, (xj + 1) * P)
                acc = psum.tile([P, D], F32, name="acc", bufs=2)
                nc.tensor.matmul_mx(
                    out=acc[:],
                    lhsT=xg[xi][0][:, cols].bitcast(FP8X4),
                    lhsT_scale=xg[xi][1][:, cols],
                    rhs=w1w[wi][:, wj, :].bitcast(FP4X4),
                    rhs_scale=w1s[wi][:, wj, :],
                    start=True,
                    stop=True,
                )
                c_rows = ring.tile([P, 2, P, 2], BF16, name="c_rows")
                c_row_words = c_rows[:].rearrange("s u p h -> s (u p h)").bitcast(F32)
                sums = acc[:].rearrange("s (p u h) -> s u p h", u=2, h=2)
                step = 1 if e == 0 else 2
                for u0 in range(0, 2, step):
                    part = slice(u0, u0 + step)
                    nc.scalar.activation(c_rows[:, part], sums[:, part], COPY, scale=gate_cols[0][:, e : e + 1])
                    turned = psum.tile([P, 4, P], F32, name="turned")
                    for u in range(u0, u0 + step):
                        nc.tensor.transpose(turned[:, u, :], c_row_words[:, u * P : (u + 1) * P], ident[:])
                    nc.scalar.copy(slot_pairs[:, part, j * P : (j + 1) * P], turned[:, part, :])
            for u in range(2):
                nc.vector.tensor_copy(c_pairs[u][:].indirect(entries(list1, first, n)), slot_pairs[:, u, :])

        load_gate(1, gate2)
        w2w = keep.tile([P, E2, 2 * D], U8, name="w2w", align_bytes=64)
        load_weights(w2w, w2_words, 0, E2)

        c_groups = runs(C_GATHERS)
        cq = []
        staged = {}

        def quantize_c(g, grouped):
            n = c_groups[g][1]
            codes = keep.tile([P, n * P], U32, name=f"c_codes{g}", align_bytes=64)
            scales = keep.tile([P, n * P], U8, name=f"c_scales{g}", align_bytes=64)
            nc.vector.quantize_mx(out=codes[:].bitcast(FP8X4), scales=scales[:], in_=grouped[:])
            cq.append((codes, scales))

        for g, (first, n) in enumerate(c_groups):
            windows = [c_pairs[u][:].bitcast(U32).indirect(entries(list2, first, n)) for u in range(2)]
            if g < EARLY:
                grouped = ring.tile([P, n * P * 4], BF16, name="c_grouped", tag="c_gathered", align_bytes=64)
                grouped_words = grouped[:].bitcast(U32).rearrange("p (m u) -> p m u", u=2)
                for u in range(2):
                    nc.vector.tensor_copy(grouped_words[:, :, u], windows[u])
                quantize_c(g, grouped)
            else:
                staged[g] = ring.tile([P, 2, n * P], U32, name="c_staged", tag="c_gathered", align_bytes=64)
                for u in range(2):
                    nc.vector.tensor_copy(staged[g][:, u, :], windows[u])

        y_tokens = [keep.tile([P, T], F32, name=f"y_tokens{t}") for t in range(4)]
        y_slots = keep.tile([P, 4, T], F32, name="y_slots")

        def scatter_y(t, first, n):
            nc.vector.tensor_copy(y_tokens[t][:].indirect(entries(list2, first, n)), y_slots[:, t, first * P : (first + n) * P])

        for b in range(BLOCKS):
            f = b * E2 // BLOCKS
            ci, cj = find(c_groups, b)
            cols = slice(cj * P, (cj + 1) * P)
            acc = psum.tile([P, D], F32, name="acc", bufs=2)
            nc.tensor.matmul_mx(
                out=acc[:],
                lhsT=cq[ci][0][:, cols].bitcast(FP8X4),
                lhsT_scale=cq[ci][1][:, cols],
                rhs=w2w[:, f, :].bitcast(FP4X4),
                rhs_scale=w2s[:, f, :],
                start=True,
                stop=True,
            )
            sums = acc[:].rearrange("s (p t) -> s t p", t=4)
            step = 1 if b == 0 else 4
            for t0 in range(0, 4, step):
                part = slice(t0, t0 + step)
                if b == 0:
                    y_rows = keep.tile([P, step, P], F32, name="y_row", tag=f"y_row{t0}", align_bytes=64)
                else:
                    y_rows = ring.tile([P, step, P], F32, name="y_rows")
                nc.scalar.activation(y_rows[:], sums[:, part], COPY, scale=gate_cols[1][:, b : b + 1])
                turned = psum.tile([P, 4, P], F32, name="turned")
                for t in range(step):
                    nc.tensor.transpose(turned[:, t, :], y_rows[:, t, :], ident[:])
                nc.scalar.copy(y_slots[:, part, b * P : (b + 1) * P], turned[:, 0:step, :])
                if b == 0 and t0 == 1:
                    woven = keep.tile([P, c_groups[EARLY][1] * P * 4], BF16, name="c_woven", tag="y_row1", align_bytes=64)
                    nc.scalar.copy(
                        woven[:].bitcast(U32).rearrange("p (m u) -> p m u", u=2), staged[EARLY][:].rearrange("p u m -> p m u")
                    )
                    quantize_c(EARLY, woven)
            for t in range(4):
                if b < SINGLY[t]:
                    scatter_y(t, b, 1)
        for t in range(4):
            scatter_y(t, SINGLY[t], BLOCKS - SINGLY[t])

        pieces = T // OUT_COLS
        out_rows = out_0.rearrange("(p t) c -> p t c", t=4)
        out_grouped = [keep.tile([P, OUT_COLS, 4], BF16, name=f"out_grouped{k}", align_bytes=64) for k in range(pieces)]
        out_scales = keep.tile([P, T], U8, name="out_scales", align_bytes=64)
        for t in range(4):
            nc.sync.dma_start(out_rows[:, t, :], y_tokens[t][:])
            for k in range(pieces):
                src = y_tokens[t][:, k * OUT_COLS : (k + 1) * OUT_COLS]
                if t == 3 and k < pieces - 1:
                    nc.vector.tensor_copy(out_grouped[k][:, :, t], src)
                elif t == 2 and k < pieces - 1:
                    nc.scalar.copy(out_grouped[k][:, :, 2:4], src.unsqueeze(2).to_broadcast([P, OUT_COLS, 2]))
                else:
                    nc.scalar.copy(out_grouped[k][:, :, t], src)
        out_words = out_1[0].rearrange("p c d -> p (c d)").bitcast(I32)
        for k in range(pieces):
            cols = slice(k * OUT_COLS, (k + 1) * OUT_COLS)
            codes = keep.tile([P, OUT_COLS], U32, name=f"out_codes{k}", align_bytes=64)
            nc.vector.quantize_mx(
                out=codes[:].bitcast(FP8X4), scales=out_scales[:, cols], in_=out_grouped[k][:].rearrange("p c t -> p (c t)")
            )
            nc.sync.dma_start(out_words[:, cols], codes[:].bitcast(I32))
        for q in range(4):
            queue = nc.sync if q == 3 else nc.scalar
            queue.dma_start(out_2[0, 4 * q : 4 * q + 4, :].bitcast(I32), out_scales[32 * q : 32 * q + 4, :].bitcast(I32))
